import numpy as np
import ml_dtypes


def mxq(x, axis, fmt="e4m3"):
    dtype, down = {"e4m3": (ml_dtypes.float8_e4m3fn, 7), "e5m2": (ml_dtypes.float8_e5m2, 14)}[fmt]
    v = np.moveaxis(np.asarray(x, np.float32).astype(ml_dtypes.bfloat16).astype(np.float64), axis, -1)
    blocks = v.reshape(v.shape[:-1] + (-1, 32))
    amax = np.abs(blocks).max(-1, keepdims=True)
    byte = np.maximum(np.where(amax > 0, np.frexp(amax)[1] - 1 + 127, 0) - down, 1)
    scale = np.exp2(byte - 127.0)
    codes = (blocks / scale).astype(np.float32).astype(dtype).astype(np.float64)
    return np.moveaxis((codes * scale).reshape(v.shape), -1, axis)


WIDE = False


def mx_kscale(k):
    if not WIDE:
        return np.ones(k)
    levels = np.array([18, -18])
    if k % 512:
        return np.exp2(np.random.permutation(np.resize(levels, k // 32))).repeat(32)
    a = np.empty((k // 512, 16))
    for p in range(k // 512):
        a[p, :8] = np.random.permutation(np.resize(levels, 8))
        for g in range(8):
            far = levels[np.abs(levels - a[p, g]) >= 10]
            a[p, g + 8] = far[np.random.randint(len(far))]
    return np.exp2(a.ravel()).repeat(32)


def f64(x):
    return np.asarray(x).astype(np.float64)


def striped(idx):
    return np.tile(np.asarray(idx).reshape(-1, 16).T, (8, 1)).astype(np.uint16)


def unstriped(offs):
    return offs[:16].T.reshape(-1).astype(np.int64)


def setup_inputs():
    n = np.random.standard_normal
    uni = np.random.uniform
    idx = np.random.permutation(2048)[:512]
    f_i = np.ones(2048)
    f_i[idx] = mx_kscale(512)
    return {
        "dy": (np.round(n((512, 512)) * 8) / 8 * f_i[idx][None, :]).astype(np.float32),
        "x": (np.round(n((512, 512)) * 8) / 8).astype(np.float32),
        "cT": (n((512, 2048)) / f_i[None, :]).astype(np.float32),
        "offs": striped(idx),
    }


def reference(dy, x, cT, offs):
    idx = unstriped(offs)
    cT_i = f64(cT)[:, idx]
    dg = f64(dy) * f64(x)
    q_cT_i = mxq(cT_i, 1, "e4m3")
    out_0 = mxq(dg, 1, "e5m2") @ q_cT_i.T
    out_1 = mxq(f64(dy), 1, "e5m2") @ q_cT_i.T
    return out_0, out_1

@@ -1,0 +1,184 @@
+from contextlib import ExitStack
+
+import concourse.mybir as mybir
+from concourse.masks import make_identity
+
+F32 = mybir.dt.float32
+BF16 = mybir.dt.bfloat16
+U32 = mybir.dt.uint32
+U16 = mybir.dt.uint16
+U8 = mybir.dt.uint8
+E4M3 = mybir.dt.float8_e4m3fn_x4
+E5M2 = mybir.dt.float8_e5m2_x4
+MULT = mybir.AluOpType.mult
+
+P = 128
+S = 512
+T = 2048
+D = 512
+FLOPS = 2 * 2 * 512 * 512 * 512
+
+
+def tile_attend_gfilm_W_kernel(tc, dy, x, cT, offs, out_0, out_1):
+    nc = tc.nc
+    with ExitStack() as ctx:
+        keep = ctx.enter_context(tc.tile_pool(name="keep", bufs=1))
+        turn = ctx.enter_context(tc.psum_pool(name="turn", bufs=3))
+        acc = ctx.enter_context(tc.psum_pool(name="acc", bufs=5))
+
+        dy_v = dy.rearrange("(p j) i -> p j i", j=4)
+        x_v = x.rearrange("(p j) i -> p j i", j=4)
+        outs = {"g": out_0.rearrange("(p j) d -> p j d", j=4), "y": out_1.rearrange("(p j) d -> p j d", j=4)}
+        eng = {"V": nc.vector.tensor_copy, "S": nc.scalar.copy}
+
+        offsets = keep.tile([P, S // 16], U16, name="offsets")
+        table = [keep.tile([P, T], F32, name=f"table{b}") for b in range(4)]
+        src = {}
+
+        def load(name, j0, j1):
+            t = keep.tile([P, j1 - j0, S], F32, name=f"{name}{j0}")
+            nc.sync.dma_start(out=t[:], in_={"dy": dy_v, "x": x_v}[name][:, j0:j1, :])
+            for j in range(j0, j1):
+                src[name, j] = t[:, j - j0, :].rearrange("p (b u r) -> p u b r", u=2, r=16)
+
+        def load_table(b):
+            nc.sync.dma_start(out=table[b][:], in_=cT[b * P : (b + 1) * P, :])
+
+        load_table(0)
+        nc.sync.dma_start(out=offsets[:], in_=offs)
+        load_table(1)
+        load_table(2)
+        load("dy", 0, 2)
+        load_table(3)
+        load("x", 0, 2)
+        load("dy", 2, 4)
+        load("x", 2, 4)
+
+        ident = keep.tile([P, P], F32, name="ident")
+        make_identity(nc, ident[:])
+
+        c_codes = keep.tile([P, D], U32, name="c_codes", align_bytes=64)
+        c_scales = keep.tile([P, D], U8, name="c_scales", align_bytes=64)
+        rows = {}
+        grouped = {}
+        quant = {}
+        sums = {}
+        res = {}
+
+        def gather(b):
+            t = keep.tile([P, 2, 16, 16], BF16, name=f"gathered{b}", align_bytes=64)
+            nc.vector.tensor_copy(out=t[:].rearrange("p u b r -> p b u r"), in_=table[b][:].indirect(offsets[:]))
+            rows["c", b] = t
+
+        def cast(j, e):
+            t = keep.tile([P, 2, 16, 16], BF16, name=f"y{j}", align_bytes=64)
+            eng[e](out=t[:], in_=src["dy", j])
+            rows["y", j] = t
+
+        def product(j):
+            t = keep.tile([P, 2, 16, 16], BF16, name=f"g{j}", align_bytes=64)
+            nc.vector.tensor_tensor(out=t[:], in0=src["dy", j], in1=src["x", j], op=MULT)
+            rows["g", j] = t
+
+        def turn_over(keys, e):
+            n = len(keys)
+            bank = turn.tile([P, n, 2, P], F32, name="bank", tag="bank")
+            for a, key in enumerate(keys):
+                words = rows[key][:].rearrange("p u b r -> p (u b r)").bitcast(F32)
+                for u in range(2):
+                    nc.tensor.transpose(bank[:, a, u, :], words[:, u * P : (u + 1) * P], ident[:])
+            name = "".join(f"{k}{j}" for k, j in keys)
+            t = keep.tile([P, n * S], BF16, name=f"grouped_{name}", align_bytes=64)
+            eng[e](
+                out=t[:].bitcast(F32).rearrange("p (a r u) -> p a r u", a=n, u=2),
+                in_=bank[:].rearrange("p a u r -> p a r u"),
+            )
+            grouped[tuple(keys)] = t
+
+        def quantize_c(b):
+            cols = slice(b * P, (b + 1) * P)
+            nc.vector.quantize_mx(out=c_codes[:, cols].bitcast(E4M3), scales=c_scales[:, cols], in_=grouped[(("c", b),)][:])
+
+        def quantize(keys):
+            n = len(keys)
+            name = "".join(f"{k}{j}" for k, j in keys)
+            codes = keep.tile([P, n * P], U32, name=f"codes_{name}", align_bytes=64)
+            scales = keep.tile([P, n * P], U8, name=f"scales_{name}", align_bytes=64)
+            nc.vector.quantize_mx(out=codes[:].bitcast(E5M2), scales=scales[:], in_=grouped[tuple(keys)][:])
+            for a, key in enumerate(keys):
+                quant[key] = (codes[:, a * P : (a + 1) * P], scales[:, a * P : (a + 1) * P])
+
+        def multiply(key):
+            codes, scales = quant[key]
+            bank = acc.tile([P, D], F32, name="sums", tag="sums")
+            nc.tensor.matmul_mx(
+                out=bank[:], lhsT=codes.bitcast(E5M2), lhsT_scale=scales,
+                rhs=c_codes[:].bitcast(E4M3), rhs_scale=c_scales[:], start=True, stop=True,
+            )
+            sums[key] = bank
+
+        def result(k, j0, j1):
+            t = keep.tile([P, j1 - j0, D], F32, name=f"res_{k}{j0}")
+            for j in range(j0, j1):
+                res[k, j] = t[:, j - j0, :]
+            return t
+
+        def drain(key, e):
+            eng[e](out=res[key], in_=sums[key][:])
+
+        def store(k, j0, j1, t):
+            nc.sync.dma_start(out=outs[k][:, j0:j1, :], in_=t[:])
+
+        for b in range(3):
+            gather(b)
+            turn_over([("c", b)], "S")
+            quantize_c(b)
+        cast(0, "V")
+        cast(1, "V")
+        turn_over([("y", 0), ("y", 1)], "S")
+        quantize([("y", 0), ("y", 1)])
+        gather(3)
+        turn_over([("c", 3)], "S")
+        product(0)
+        product(1)
+        quantize_c(3)
+        turn_over([("g", 0), ("g", 1)], "S")
+        ry0 = result("y", 0, 1)
+        ry1 = result("y", 1, 2)
+        rg01 = result("g", 0, 2)
+        ry23 = result("y", 2, 4)
+        rg2 = result("g", 2, 3)
+        rg3 = result("g", 3, 4)
+        multiply(("y", 0))
+        multiply(("y", 1))
+        cast(2, "V")
+        cast(3, "V")
+        drain(("y", 0), "S")
+        store("y", 0, 1, ry0)
+        quantize([("g", 0), ("g", 1)])
+        turn_over([("y", 2), ("y", 3)], "S")
+        drain(("y", 1), "S")
+        store("y", 1, 2, ry1)
+        product(2)
+        product(3)
+        multiply(("g", 0))
+        multiply(("g", 1))
+        quantize([("y", 2), ("y", 3)])
+        turn_over([("g", 2)], "V")
+        turn_over([("g", 3)], "V")
+        drain(("g", 0), "S")
+        drain(("g", 1), "S")
+        store("g", 0, 2, rg01)
+        multiply(("y", 2))
+        multiply(("y", 3))
+        quantize([("g", 2)])
+        quantize([("g", 3)])
+        drain(("y", 2), "S")
+        drain(("y", 3), "V")
+        store("y", 2, 4, ry23)
+        multiply(("g", 2))
+        multiply(("g", 3))
+        drain(("g", 2), "S")
+        store("g", 2, 3, rg2)
+        drain(("g", 3), "V")
+        store("g", 3, 4, rg3)

@@ -23,6 +23,7 @@ def tile_attend_gfilm_W_kernel(tc, dy, x, cT, offs, out_0, out_1):
     nc = tc.nc
     with ExitStack() as ctx:
         keep = ctx.enter_context(tc.tile_pool(name="keep", bufs=1))
+        late = ctx.enter_context(tc.tile_pool(name="late", bufs=1))
         turn = ctx.enter_context(tc.psum_pool(name="turn", bufs=3))
         acc = ctx.enter_context(tc.psum_pool(name="acc", bufs=5))
 
@@ -32,11 +33,23 @@ def tile_attend_gfilm_W_kernel(tc, dy, x, cT, offs, out_0, out_1):
         eng = {"V": nc.vector.tensor_copy, "S": nc.scalar.copy}
 
         offsets = keep.tile([P, S // 16], U16, name="offsets")
-        table = [keep.tile([P, T], F32, name=f"table{b}") for b in range(4)]
+        table = [keep.tile([P, T], F32, name=f"table{b}") for b in range(2)]
+        table.append(late.tile([P, T], F32, name="table2", align_bytes=64, offset=8192))
+        table.append(late.tile([P, T], F32, name="table3", align_bytes=64, offset=0))
+        place = {("y", 2): 0, ("y", 3): 1024, "codes_g0g1": 4096, ("g", 2): 2048, ("g", 3): 3072, "c3": 2560, ("g", 0): 8192, ("g", 1): 9216, "c2": 16384, ("c", 3): 16384, "x0": 24576, "codes_y0y1": 24576}
+
+        def row_tile(k, j):
+            if (k, j) in place:
+                return late.tile([P, 2, 16, 16], BF16, name=f"{k}{j}", align_bytes=64, offset=place[k, j])
+            return keep.tile([P, 2, 16, 16], BF16, name=f"{k}{j}", align_bytes=64)
+
         src = {}
 
         def load(name, j0, j1):
-            t = keep.tile([P, j1 - j0, S], F32, name=f"{name}{j0}")
+            if f"{name}{j0}" in place:
+                t = late.tile([P, j1 - j0, S], F32, name=f"{name}{j0}", align_bytes=64, offset=place[f"{name}{j0}"])
+            else:
+                t = keep.tile([P, j1 - j0, S], F32, name=f"{name}{j0}")
             nc.sync.dma_start(out=t[:], in_={"dy": dy_v, "x": x_v}[name][:, j0:j1, :])
             for j in range(j0, j1):
                 src[name, j] = t[:, j - j0, :].rearrange("p (b u r) -> p u b r", u=2, r=16)
@@ -46,19 +59,21 @@ def tile_attend_gfilm_W_kernel(tc, dy, x, cT, offs, out_0, out_1):
 
         load_table(0)
         nc.sync.dma_start(out=offsets[:], in_=offs)
+        load("dy", 0, 2)
         load_table(1)
         load_table(2)
-        load("dy", 0, 2)
-        load_table(3)
         load("x", 0, 2)
+        load_table(3)
         load("dy", 2, 4)
         load("x", 2, 4)
 
         ident = keep.tile([P, P], F32, name="ident")
         make_identity(nc, ident[:])
 
-        c_codes = keep.tile([P, D], U32, name="c_codes", align_bytes=64)
-        c_scales = keep.tile([P, D], U8, name="c_scales", align_bytes=64)
+        c_codes = keep.tile([P, P + D], U32, name="c_codes", align_bytes=64)
+        c_scales = keep.tile([P, P + D], U8, name="c_scales", align_bytes=64)
+        nc.gpsimd.memset(c_codes[:, 0:P], 0)
+        nc.gpsimd.memset(c_scales[:, 0:P], 0)
         rows = {}
         grouped = {}
         quant = {}
@@ -66,17 +81,17 @@ def tile_attend_gfilm_W_kernel(tc, dy, x, cT, offs, out_0, out_1):
         res = {}
 
         def gather(b):
-            t = keep.tile([P, 2, 16, 16], BF16, name=f"gathered{b}", align_bytes=64)
+            t = row_tile("c", b)
             nc.vector.tensor_copy(out=t[:].rearrange("p u b r -> p b u r"), in_=table[b][:].indirect(offsets[:]))
             rows["c", b] = t
 
         def cast(j, e):
-            t = keep.tile([P, 2, 16, 16], BF16, name=f"y{j}", align_bytes=64)
+            t = row_tile("y", j)
             eng[e](out=t[:], in_=src["dy", j])
             rows["y", j] = t
 
         def product(j):
-            t = keep.tile([P, 2, 16, 16], BF16, name=f"g{j}", align_bytes=64)
+            t = row_tile("g", j)
             nc.vector.tensor_tensor(out=t[:], in0=src["dy", j], in1=src["x", j], op=MULT)
             rows["g", j] = t
 
@@ -88,7 +103,10 @@ def tile_attend_gfilm_W_kernel(tc, dy, x, cT, offs, out_0, out_1):
                 for u in range(2):
                     nc.tensor.transpose(bank[:, a, u, :], words[:, u * P : (u + 1) * P], ident[:])
             name = "".join(f"{k}{j}" for k, j in keys)
-            t = keep.tile([P, n * S], BF16, name=f"grouped_{name}", align_bytes=64)
+            if name in place:
+                t = late.tile([P, n * S], BF16, name=f"grouped_{name}", align_bytes=64, offset=place[name])
+            else:
+                t = keep.tile([P, n * S], BF16, name=f"grouped_{name}", align_bytes=64)
             eng[e](
                 out=t[:].bitcast(F32).rearrange("p (a r u) -> p a r u", a=n, u=2),
                 in_=bank[:].rearrange("p a u r -> p a r u"),
@@ -96,24 +114,27 @@ def tile_attend_gfilm_W_kernel(tc, dy, x, cT, offs, out_0, out_1):
             grouped[tuple(keys)] = t
 
         def quantize_c(b):
-            cols = slice(b * P, (b + 1) * P)
+            cols = slice((b + 1) * P, (b + 2) * P)
             nc.vector.quantize_mx(out=c_codes[:, cols].bitcast(E4M3), scales=c_scales[:, cols], in_=grouped[(("c", b),)][:])
 
         def quantize(keys):
             n = len(keys)
             name = "".join(f"{k}{j}" for k, j in keys)
-            codes = keep.tile([P, n * P], U32, name=f"codes_{name}", align_bytes=64)
+            if f"codes_{name}" in place:
+                codes = late.tile([P, n * P], U32, name=f"codes_{name}", align_bytes=64, offset=place[f"codes_{name}"])
+            else:
+                codes = keep.tile([P, n * P], U32, name=f"codes_{name}", align_bytes=64)
             scales = keep.tile([P, n * P], U8, name=f"scales_{name}", align_bytes=64)
             nc.vector.quantize_mx(out=codes[:].bitcast(E5M2), scales=scales[:], in_=grouped[tuple(keys)][:])
             for a, key in enumerate(keys):
                 quant[key] = (codes[:, a * P : (a + 1) * P], scales[:, a * P : (a + 1) * P])
 
-        def multiply(key):
+        def multiply(key, first=P):
             codes, scales = quant[key]
             bank = acc.tile([P, D], F32, name="sums", tag="sums")
             nc.tensor.matmul_mx(
                 out=bank[:], lhsT=codes.bitcast(E5M2), lhsT_scale=scales,
-                rhs=c_codes[:].bitcast(E4M3), rhs_scale=c_scales[:], start=True, stop=True,
+                rhs=c_codes[:, first : first + D].bitcast(E4M3), rhs_scale=c_scales[:, first : first + D], start=True, stop=True,
             )
             sums[key] = bank
 
@@ -123,62 +144,64 @@ def tile_attend_gfilm_W_kernel(tc, dy, x, cT, offs, out_0, out_1):
                 res[k, j] = t[:, j - j0, :]
             return t
 
+        def part(k, j0, j1, d0, d1, first, engines):
+            t = keep.tile([P, j1 - j0, d1 - d0], F32, name=f"part_{k}{j0}_{d0}")
+            for j in range(j0, j1):
+                eng[engines[j - j0]](out=t[:, j - j0, :], in_=sums[k, j][:, d0 + P - first : d1 + P - first])
+            nc.sync.dma_start(out=outs[k][:, j0:j1, d0:d1], in_=t[:])
+            return t
+
         def drain(key, e):
             eng[e](out=res[key], in_=sums[key][:])
 
         def store(k, j0, j1, t):
             nc.sync.dma_start(out=outs[k][:, j0:j1, :], in_=t[:])
 
-        for b in range(3):
-            gather(b)
-            turn_over([("c", b)], "S")
-            quantize_c(b)
+        gather(0)
+        turn_over([("c", 0)], "S")
+        quantize_c(0)
         cast(0, "V")
         cast(1, "V")
         turn_over([("y", 0), ("y", 1)], "S")
-        quantize([("y", 0), ("y", 1)])
-        gather(3)
-        turn_over([("c", 3)], "S")
+        gather(1)
+        turn_over([("c", 1)], "S")
+        quantize_c(1)
+        gather(2)
+        turn_over([("c", 2)], "S")
         product(0)
         product(1)
-        quantize_c(3)
+        quantize_c(2)
+        quantize([("y", 0), ("y", 1)])
         turn_over([("g", 0), ("g", 1)], "S")
-        ry0 = result("y", 0, 1)
-        ry1 = result("y", 1, 2)
-        rg01 = result("g", 0, 2)
-        ry23 = result("y", 2, 4)
-        rg2 = result("g", 2, 3)
-        rg3 = result("g", 3, 4)
-        multiply(("y", 0))
-        multiply(("y", 1))
+        gather(3)
+        turn_over([("c", 3)], "S")
+        multiply(("y", 0), 0)
+        e0 = part("y", 0, 1, 0, 384, 0, "S")
+        multiply(("y", 1), 0)
+        part("y", 1, 2, 0, 384, 0, "S")
         cast(2, "V")
         cast(3, "V")
-        drain(("y", 0), "S")
-        store("y", 0, 1, ry0)
+        quantize_c(3)
         quantize([("g", 0), ("g", 1)])
         turn_over([("y", 2), ("y", 3)], "S")
-        drain(("y", 1), "S")
-        store("y", 1, 2, ry1)
+        multiply(("g", 0))
+        e1 = part("g", 0, 1, 0, 512, P, "S")
+        multiply(("g", 1))
+        part("g", 1, 2, 0, 512, P, "S")
         product(2)
         product(3)
-        multiply(("g", 0))
-        multiply(("g", 1))
         quantize([("y", 2), ("y", 3)])
         turn_over([("g", 2)], "V")
         turn_over([("g", 3)], "V")
-        drain(("g", 0), "S")
-        drain(("g", 1), "S")
-        store("g", 0, 2, rg01)
-        multiply(("y", 2))
-        multiply(("y", 3))
         quantize([("g", 2)])
         quantize([("g", 3)])
-        drain(("y", 2), "S")
-        drain(("y", 3), "V")
-        store("y", 2, 4, ry23)
+        multiply(("y", 2))
+        part("y", 2, 3, 0, 512, P, "S")
+        multiply(("y", 3))
+        part("y", 3, 4, 0, 512, P, "S")
         multiply(("g", 2))
         multiply(("g", 3))
-        drain(("g", 2), "S")
-        store("g", 2, 3, rg2)
-        drain(("g", 3), "V")
-        store("g", 3, 4, rg3)
+        part("g", 2, 4, 0, 512, P, "VS")
+        multiply(("y", 0))
+        multiply(("y", 1))
+        part("y", 0, 2, 384, 512, P, "VV")

from contextlib import ExitStack

import concourse.mybir as mybir
from concourse.masks import make_identity

F32 = mybir.dt.float32
BF16 = mybir.dt.bfloat16
U32 = mybir.dt.uint32
U16 = mybir.dt.uint16
U8 = mybir.dt.uint8
E4M3 = mybir.dt.float8_e4m3fn_x4
E5M2 = mybir.dt.float8_e5m2_x4
MULT = mybir.AluOpType.mult

P = 128
S = 512
T = 2048
D = 512
FLOPS = 2 * 2 * 512 * 512 * 512


def tile_attend_gfilm_W_kernel(tc, dy, x, cT, offs, out_0, out_1):
    nc = tc.nc
    with ExitStack() as ctx:
        keep = ctx.enter_context(tc.tile_pool(name="keep", bufs=1))
        late = ctx.enter_context(tc.tile_pool(name="late", bufs=1))
        turn = ctx.enter_context(tc.psum_pool(name="turn", bufs=3))
        acc = ctx.enter_context(tc.psum_pool(name="acc", bufs=5))

        dy_v = dy.rearrange("(p j) i -> p j i", j=4)
        x_v = x.rearrange("(p j) i -> p j i", j=4)
        outs = {"g": out_0.rearrange("(p j) d -> p j d", j=4), "y": out_1.rearrange("(p j) d -> p j d", j=4)}
        eng = {"V": nc.vector.tensor_copy, "S": nc.scalar.copy}

        offsets = keep.tile([P, S // 16], U16, name="offsets")
        table = [keep.tile([P, T], F32, name=f"table{b}") for b in range(2)]
        table.append(late.tile([P, T], F32, name="table2", align_bytes=64, offset=8192))
        table.append(late.tile([P, T], F32, name="table3", align_bytes=64, offset=0))
        place = {("y", 2): 0, ("y", 3): 1024, "codes_g0g1": 4096, ("g", 2): 2048, ("g", 3): 3072, "c3": 2560, ("g", 0): 8192, ("g", 1): 9216, "c2": 16384, ("c", 3): 16384, "x0": 24576, "codes_y0y1": 24576}

        def row_tile(k, j):
            if (k, j) in place:
                return late.tile([P, 2, 16, 16], BF16, name=f"{k}{j}", align_bytes=64, offset=place[k, j])
            return keep.tile([P, 2, 16, 16], BF16, name=f"{k}{j}", align_bytes=64)

        src = {}

        def load(name, j0, j1):
            if f"{name}{j0}" in place:
                t = late.tile([P, j1 - j0, S], F32, name=f"{name}{j0}", align_bytes=64, offset=place[f"{name}{j0}"])
            else:
                t = keep.tile([P, j1 - j0, S], F32, name=f"{name}{j0}")
            nc.sync.dma_start(out=t[:], in_={"dy": dy_v, "x": x_v}[name][:, j0:j1, :])
            for j in range(j0, j1):
                src[name, j] = t[:, j - j0, :].rearrange("p (b u r) -> p u b r", u=2, r=16)

        def load_table(b):
            nc.sync.dma_start(out=table[b][:], in_=cT[b * P : (b + 1) * P, :])

        load_table(0)
        nc.sync.dma_start(out=offsets[:], in_=offs)
        load("dy", 0, 2)
        load_table(1)
        load_table(2)
        load("x", 0, 2)
        load_table(3)
        load("dy", 2, 4)
        load("x", 2, 4)

        ident = keep.tile([P, P], F32, name="ident")
        make_identity(nc, ident[:])

        c_codes = keep.tile([P, P + D], U32, name="c_codes", align_bytes=64)
        c_scales = keep.tile([P, P + D], U8, name="c_scales", align_bytes=64)
        nc.gpsimd.memset(c_codes[:, 0:P], 0)
        nc.gpsimd.memset(c_scales[:, 0:P], 0)
        rows = {}
        grouped = {}
        quant = {}
        sums = {}
        res = {}

        def gather(b):
            t = row_tile("c", b)
            nc.vector.tensor_copy(out=t[:].rearrange("p u b r -> p b u r"), in_=table[b][:].indirect(offsets[:]))
            rows["c", b] = t

        def cast(j, e):
            t = row_tile("y", j)
            eng[e](out=t[:], in_=src["dy", j])
            rows["y", j] = t

        def product(j):
            t = row_tile("g", j)
            nc.vector.tensor_tensor(out=t[:], in0=src["dy", j], in1=src["x", j], op=MULT)
            rows["g", j] = t

        def turn_over(keys, e):
            n = len(keys)
            bank = turn.tile([P, n, 2, P], F32, name="bank", tag="bank")
            for a, key in enumerate(keys):
                words = rows[key][:].rearrange("p u b r -> p (u b r)").bitcast(F32)
                for u in range(2):
                    nc.tensor.transpose(bank[:, a, u, :], words[:, u * P : (u + 1) * P], ident[:])
            name = "".join(f"{k}{j}" for k, j in keys)
            if name in place:
                t = late.tile([P, n * S], BF16, name=f"grouped_{name}", align_bytes=64, offset=place[name])
            else:
                t = keep.tile([P, n * S], BF16, name=f"grouped_{name}", align_bytes=64)
            eng[e](
                out=t[:].bitcast(F32).rearrange("p (a r u) -> p a r u", a=n, u=2),
                in_=bank[:].rearrange("p a u r -> p a r u"),
            )
            grouped[tuple(keys)] = t

        def quantize_c(b):
            cols = slice((b + 1) * P, (b + 2) * P)
            nc.vector.quantize_mx(out=c_codes[:, cols].bitcast(E4M3), scales=c_scales[:, cols], in_=grouped[(("c", b),)][:])

        def quantize(keys):
            n = len(keys)
            name = "".join(f"{k}{j}" for k, j in keys)
            if f"codes_{name}" in place:
                codes = late.tile([P, n * P], U32, name=f"codes_{name}", align_bytes=64, offset=place[f"codes_{name}"])
            else:
                codes = keep.tile([P, n * P], U32, name=f"codes_{name}", align_bytes=64)
            scales = keep.tile([P, n * P], U8, name=f"scales_{name}", align_bytes=64)
            nc.vector.quantize_mx(out=codes[:].bitcast(E5M2), scales=scales[:], in_=grouped[tuple(keys)][:])
            for a, key in enumerate(keys):
                quant[key] = (codes[:, a * P : (a + 1) * P], scales[:, a * P : (a + 1) * P])

        def multiply(key, first=P):
            codes, scales = quant[key]
            bank = acc.tile([P, D], F32, name="sums", tag="sums")
            nc.tensor.matmul_mx(
                out=bank[:], lhsT=codes.bitcast(E5M2), lhsT_scale=scales,
                rhs=c_codes[:, first : first + D].bitcast(E4M3), rhs_scale=c_scales[:, first : first + D], start=True, stop=True,
            )
            sums[key] = bank

        def result(k, j0, j1):
            t = keep.tile([P, j1 - j0, D], F32, name=f"res_{k}{j0}")
            for j in range(j0, j1):
                res[k, j] = t[:, j - j0, :]
            return t

        def part(k, j0, j1, d0, d1, first, engines):
            t = keep.tile([P, j1 - j0, d1 - d0], F32, name=f"part_{k}{j0}_{d0}")
            for j in range(j0, j1):
                eng[engines[j - j0]](out=t[:, j - j0, :], in_=sums[k, j][:, d0 + P - first : d1 + P - first])
            nc.sync.dma_start(out=outs[k][:, j0:j1, d0:d1], in_=t[:])
            return t

        def drain(key, e):
            eng[e](out=res[key], in_=sums[key][:])

        def store(k, j0, j1, t):
            nc.sync.dma_start(out=outs[k][:, j0:j1, :], in_=t[:])

        gather(0)
        turn_over([("c", 0)], "S")
        quantize_c(0)
        cast(0, "V")
        cast(1, "V")
        turn_over([("y", 0), ("y", 1)], "S")
        gather(1)
        turn_over([("c", 1)], "S")
        quantize_c(1)
        gather(2)
        turn_over([("c", 2)], "S")
        product(0)
        product(1)
        quantize_c(2)
        quantize([("y", 0), ("y", 1)])
        turn_over([("g", 0), ("g", 1)], "S")
        gather(3)
        turn_over([("c", 3)], "S")
        multiply(("y", 0), 0)
        e0 = part("y", 0, 1, 0, 384, 0, "S")
        multiply(("y", 1), 0)
        part("y", 1, 2, 0, 384, 0, "S")
        cast(2, "V")
        cast(3, "V")
        quantize_c(3)
        quantize([("g", 0), ("g", 1)])
        turn_over([("y", 2), ("y", 3)], "S")
        multiply(("g", 0))
        e1 = part("g", 0, 1, 0, 512, P, "S")
        multiply(("g", 1))
        part("g", 1, 2, 0, 512, P, "S")
        product(2)
        product(3)
        quantize([("y", 2), ("y", 3)])
        turn_over([("g", 2)], "V")
        turn_over([("g", 3)], "V")
        quantize([("g", 2)])
        quantize([("g", 3)])
        multiply(("y", 2))
        part("y", 2, 3, 0, 512, P, "S")
        multiply(("y", 3))
        part("y", 3, 4, 0, 512, P, "S")
        multiply(("g", 2))
        multiply(("g", 3))
        part("g", 2, 4, 0, 512, P, "VS")
        multiply(("y", 0))
        multiply(("y", 1))
        part("y", 0, 2, 384, 512, P, "VV")
